import numpy as np
import ml_dtypes


def mxq(x, axis, fmt="e4m3"):
    dtype, down = {"e4m3": (ml_dtypes.float8_e4m3fn, 7), "e5m2": (ml_dtypes.float8_e5m2, 14)}[fmt]
    v = np.moveaxis(np.asarray(x, np.float32).astype(ml_dtypes.bfloat16).astype(np.float64), axis, -1)
    blocks = v.reshape(v.shape[:-1] + (-1, 32))
    amax = np.abs(blocks).max(-1, keepdims=True)
    byte = np.maximum(np.where(amax > 0, np.frexp(amax)[1] - 1 + 127, 0) - down, 1)
    scale = np.exp2(byte - 127.0)
    codes = (blocks / scale).astype(np.float32).astype(dtype).astype(np.float64)
    return np.moveaxis((codes * scale).reshape(v.shape), -1, axis)


WIDE = False


def mx_kscale(k):
    if not WIDE:
        return np.ones(k)
    levels = np.array([30, -30])
    if k % 512:
        return np.exp2(np.random.permutation(np.resize(levels, k // 32))).repeat(32)
    a = np.empty((k // 512, 16))
    for p in range(k // 512):
        a[p, :8] = np.random.permutation(np.resize(levels, 8))
        for g in range(8):
            far = levels[np.abs(levels - a[p, g]) >= 10]
            a[p, g + 8] = far[np.random.randint(len(far))]
    return np.exp2(a.ravel()).repeat(32)


def f64(x):
    return np.asarray(x).astype(np.float64)


def striped(idx):
    return np.tile(np.asarray(idx).reshape(-1, 16).T, (8, 1)).astype(np.uint16)


def unstriped(offs):
    return offs[:16].T.reshape(-1).astype(np.int64)


E2M1 = np.array([0.0, 0.5, 1.0, 1.5, 2.0, 3.0, 4.0, 6.0, -0.0, -0.5, -1.0, -1.5, -2.0, -3.0, -4.0, -6.0])


def pack_weight(w, fmt):
    k, n = w.shape
    w = f64(np.asarray(w, np.float32).astype(ml_dtypes.bfloat16)).reshape(k // 32, 32, n)
    amax = np.abs(w).max(1)
    if fmt in ("e4m3", "e5m2"):
        byte = np.frexp(amax)[1] - 1 + 127 - (7 if fmt == "e4m3" else 14)
    else:
        mant, ex = np.frexp(amax / 6.0)
        byte = np.where(mant > 0.5, ex, ex - 1) + 127
    byte = np.clip(np.where(amax > 0, byte, 1), 1, 254)
    scaled = (w * np.exp2(127.0 - byte)[:, None, :]).reshape(k, n).astype(np.float32)
    by_word = np.ascontiguousarray(scaled.reshape(k // 512, 128, 4, n).transpose(0, 1, 3, 2))
    if fmt in ("e4m3", "e5m2"):
        words = by_word.astype(ml_dtypes.float8_e4m3fn if fmt == "e4m3" else ml_dtypes.float8_e5m2).view(np.uint8)
    else:
        c = by_word.astype(ml_dtypes.float4_e2m1fn).view(np.uint8) & 0xF
        words = (c[..., 0::2] | (c[..., 1::2] << 4)).reshape(k // 512, 128, 2 * n)
    return np.ascontiguousarray(words), np.ascontiguousarray(byte.astype(np.uint8).reshape(k // 512, 16, n))


def unpack_weight(words, scales, fmt):
    g, _, n = scales.shape
    words = np.ascontiguousarray(words).reshape(g, 128, n, -1)
    if fmt in ("e4m3", "e5m2"):
        vals = words.view(ml_dtypes.float8_e4m3fn if fmt == "e4m3" else ml_dtypes.float8_e5m2).astype(np.float64)
    else:
        nib = np.empty((g, 128, n, 4), np.uint8)
        nib[..., 0::2] = words & 0xF
        nib[..., 1::2] = words >> 4
        vals = E2M1[nib]
    vals = vals * np.repeat(np.exp2(scales.astype(np.float64) - 127.0), 8, axis=1)[..., None]
    return vals.transpose(0, 1, 3, 2).reshape(g * 512, n)


def sigmoid(v):
    return 1.0 / (1.0 + np.exp(-v))


def sgn(shape):
    return np.random.uniform(0.5, 2.0, shape) * np.where(np.random.standard_normal(shape) < 0, -1.0, 1.0)


K, T, J, R, O, N = 512, 1024, 256, 512, 128, 256


def setup_inputs():
    n = np.random.standard_normal
    idx = np.random.permutation(T)[:J]
    idx2 = np.random.permutation(J)[:J]
    idx3 = np.random.permutation(J)[:O]
    fk = mx_kscale(K)
    fr = mx_kscale(R)
    fr = fr / fr.max()
    xtp = pack_weight(n((K, T)) / fk[:, None], "e2m1")
    wp = pack_weight(n((K, R)) * 1 / np.sqrt(K) * fk[:, None], "e4m3")
    w2p = pack_weight(n((K, R)) * 1 / np.sqrt(K) * fk[:, None], "e5m2")
    wbp = pack_weight(n((R, N)) * 1 / np.sqrt(R) / fr[:, None], "e2m1")
    return {
        "xt_words": xtp[0],
        "xt_scales": xtp[1],
        "w_words": wp[0],
        "w_scales": wp[1],
        "w2_words": w2p[0],
        "w2_scales": w2p[1],
        "sg": (0.4 * sgn((R, 1))).astype(np.float32),
        "lo": (np.random.uniform(-2.6, -1.2, (R, 1)) + np.log(fr)[:, None]).astype(np.float32),
        "wb_words": wbp[0],
        "wb_scales": wbp[1],
        "offs": striped(idx),
        "offs2": striped(idx2),
        "offs3": striped(idx3),
    }


def reference(xt_words, xt_scales, w_words, w_scales, w2_words, w2_scales, sg, lo, wb_words, wb_scales, offs, offs2, offs3):
    idx = unstriped(offs)
    idx2 = unstriped(offs2)
    idx3 = unstriped(offs3)
    xtu = unpack_weight(xt_words, xt_scales, "e2m1")
    wu = unpack_weight(w_words, w_scales, "e4m3")
    w2u = unpack_weight(w2_words, w2_scales, "e5m2")
    wbu = unpack_weight(wb_words, wb_scales, "e2m1")
    xtidxg = xtu[:, idx]
    a = wu.T @ xtidxg
    b = w2u.T @ xtidxg
    g1 = np.maximum(a, b[:, idx2])
    hid = sigmoid(g1[:, idx3] * f64(sg) + f64(lo))
    hidq = mxq(hid, 0, "e4m3")
    p = wbu.T @ hidq
    return p

@@ -1,0 +1,175 @@
+from contextlib import ExitStack
+
+import concourse.mybir as mybir
+
+K, T, J, R, O, N = 512, 1024, 256, 512, 128, 256
+FLOPS = 2 * K * R * J * 2 + 2 * R * N * O
+
+F32 = mybir.dt.float32
+BF16 = mybir.dt.bfloat16
+I32 = mybir.dt.int32
+U32 = mybir.dt.uint32
+U16 = mybir.dt.uint16
+U8 = mybir.dt.uint8
+E4M3 = mybir.dt.float8_e4m3fn_x4
+E5M2 = mybir.dt.float8_e5m2_x4
+E2M1 = mybir.dt.float4_e2m1fn_x4
+ACT = mybir.ActivationFunctionType
+ALU = mybir.AluOpType
+
+P = 128
+PACK = 4
+HALF = J // 2
+
+
+def tile_list_partnersig_kernel(tc, xt_words, xt_scales, w_words, w_scales, w2_words, w2_scales, sg, lo,
+                                    wb_words, wb_scales, offs, offs2, offs3, out):
+    nc = tc.nc
+    with ExitStack() as ctx:
+        sb = ctx.enter_context(tc.tile_pool(name="sb", bufs=1))
+        psum = ctx.enter_context(tc.psum_pool(name="psum", bufs=1))
+
+        def plane(name, width):
+            tile_ = sb.tile([P, width], U8, name=name, align_bytes=64)
+            nc.vector.memset(tile_[:].bitcast(I32), 0)
+            return tile_
+
+        def load_plane(queue, tile_, scales):
+            for q in range(4):
+                queue.dma_start(out=tile_[32 * q : 32 * q + 4, :].bitcast(I32), in_=scales[0, 4 * q : 4 * q + 4, :].bitcast(I32))
+
+        warm_in = sb.tile([P, 1], F32, name="warm_in")
+        warm_out = sb.tile([P, 1], F32, name="warm_out")
+        nc.gpsimd.memset(warm_in[:], 0.0)
+        nc.scalar.activation(out=warm_out[:], in_=warm_in[:], func=ACT.Sigmoid)
+
+        xs = plane("xs", T)
+        w2s = plane("w2s", R)
+        ws = plane("ws", R)
+        wbs = plane("wbs", N)
+
+        list1 = sb.tile([P, J // 16], U16, name="list1")
+        list2 = sb.tile([P, J // 16], U16, name="list2")
+        list3 = sb.tile([P, O // 16], U16, name="list3")
+        xw = sb.tile([P, T], U16, name="xw", align_bytes=64)
+        ww = sb.tile([P, R], U32, name="ww", align_bytes=64)
+        w2w = sb.tile([P, R], U32, name="w2w", align_bytes=64)
+        wbw = sb.tile([P, 2 * N], U8, name="wbw", align_bytes=64)
+        slope = sb.tile([P, PACK], F32, name="slope")
+        offset = sb.tile([P, PACK], F32, name="offset")
+        w2s_rows = sb.tile([4, 4, R // 4], I32, name="w2s_rows")
+        ws_rows = sb.tile([4, 4, R // 4], I32, name="ws_rows")
+        xs_rows = sb.tile([4, 4, T // 4], I32, name="xs_rows")
+
+        nc.sync.dma_start(list1[:], offs)
+        nc.sync.dma_start(out=w2s_rows[:], in_=w2_scales[0].bitcast(I32).rearrange("(q r) c -> r q c", r=4))
+        nc.sync.dma_start(out=xw[:].bitcast(I32), in_=xt_words[0].bitcast(I32))
+        nc.sync.dma_start(out=w2w[:].bitcast(I32), in_=w2_words[0].rearrange("p c t -> p (c t)").bitcast(I32))
+        load_plane(nc.sync, xs, xt_scales)
+        nc.sync.dma_start(out=ww[:].bitcast(I32), in_=w_words[0].rearrange("p c t -> p (c t)").bitcast(I32))
+        load_plane(nc.sync, ws, w_scales)
+        nc.sync.dma_start(list2[:], offs2)
+        nc.sync.dma_start(list3[:], offs3)
+        nc.sync.dma_start(out=slope[:], in_=sg.rearrange("(p t) o -> p (t o)", t=PACK))
+        nc.sync.dma_start(out=offset[:], in_=lo.rearrange("(p t) o -> p (t o)", t=PACK))
+        nc.sync.dma_start(out=wbw[:].bitcast(I32), in_=wb_words[0].bitcast(I32))
+        load_plane(nc.sync, wbs, wb_scales)
+
+        def spread(tile_, rows):
+            for q in range(4):
+                nc.vector.tensor_copy(tile_[32 * q : 32 * q + 4, :].bitcast(I32), rows[:, q, :])
+
+        def deal(copy, name, src, dtype):
+            dealt = sb.tile([P, R], dtype, name=name, align_bytes=64)
+            copy(dealt[:].rearrange("p (t m) -> p m t", t=PACK), src[:].rearrange("p (m t) -> p m t", t=PACK))
+            return dealt
+
+        xg = sb.tile([P, J], U16, name="xg", align_bytes=64)
+        xsg = sb.tile([P, J], U8, name="xsg", align_bytes=64)
+
+        def pick(h, n):
+            cols = slice(h * J // n, (h + 1) * J // n)
+            entries = list1[:, h * 16 // n : (h + 1) * 16 // n]
+            nc.vector.tensor_copy(xg[:, cols], xw[:].indirect(entries))
+            nc.vector.tensor_copy(xsg[:, cols], xs[:].indirect(entries))
+
+        spread(w2s, w2s_rows)
+        w2s_d = deal(nc.vector.tensor_copy, "w2s_d", w2s, U8)
+        w2w_d = deal(nc.scalar.copy, "w2w_d", w2w, U32)
+        pick(0, 2)
+        pick(1, 2)
+        ww_d = deal(nc.scalar.copy, "ww_d", ww, U32)
+        ws_d = deal(nc.vector.tensor_copy, "ws_d", ws, U8)
+
+        b_ps = [psum.tile([P, J], F32, name="bank%d" % t, tag="bank%d" % t) for t in range(PACK)]
+        a_ps = [psum.tile([P, J], F32, name="bank%d" % (PACK + t), tag="bank%d" % (PACK + t)) for t in range(PACK)]
+
+        def product(acc, words, scales, fmt, t, cols):
+            rows = slice(t * P, (t + 1) * P)
+            nc.tensor.matmul_mx(out=acc[:, cols], lhsT=words[:, rows].bitcast(fmt), lhsT_scale=scales[:, rows],
+                                rhs=xg[:, cols].bitcast(E2M1), rhs_scale=xsg[:, cols], start=True, stop=True)
+
+        for h in range(2):
+            for t in range(PACK):
+                product(b_ps[t], w2w_d, w2s_d, E5M2, t, slice(h * J // 2, (h + 1) * J // 2))
+        for t in range(PACK):
+            product(a_ps[t], ww_d, ws_d, E4M3, t, slice(0, J))
+
+        b_sb = [sb.tile([P, J], F32, name="b%d" % t) for t in range(PACK)]
+        partner = [sb.tile([P, J], F32, name="partner%d" % t) for t in range(PACK)]
+        g1 = [sb.tile([P, J], F32, name="g1_%d" % t) for t in range(PACK)]
+        hid = sb.tile([P, PACK * O], BF16, name="hid", align_bytes=64)
+
+        def step(kind, t, eng):
+            if kind == "c":
+                (nc.vector.tensor_copy if eng == "V" else nc.scalar.copy)(b_sb[t][:, 0:J], b_ps[t][:])
+            elif kind in ("g", "h", "i"):
+                lo_, hi_ = {"g": (0, J), "h": (0, HALF), "i": (HALF, J)}[kind]
+                src = b_sb[t][:].indirect(list2[:, lo_ // 16 : hi_ // 16])
+                if eng == "V":
+                    nc.vector.tensor_copy(partner[t][:, lo_:hi_], src)
+                else:
+                    nc.scalar.activation(partner[t][:, lo_:hi_], src, ACT.Copy)
+            elif kind == "m":
+                nc.vector.tensor_tensor(g1[t][:], a_ps[t][:], partner[t][:], ALU.max)
+            else:
+                nc.scalar.activation(out=hid[:, t : PACK * O : PACK], in_=g1[t][:].indirect(list3[:]), func=ACT.Sigmoid,
+                                     bias=offset[:, t : t + 1], scale=slope[:, t : t + 1])
+
+        step("c", 0, "S")
+        step("c", 1, "V")
+        step("c", 2, "S")
+        step("c", 3, "V")
+        step("h", 0, "V")
+        step("i", 0, "S")
+        step("h", 1, "V")
+        step("i", 1, "S")
+        step("m", 0, "")
+        step("i", 2, "S")
+        step("h", 2, "V")
+        step("m", 1, "")
+        step("i", 3, "S")
+        step("h", 3, "V")
+        step("s", 0, "")
+        step("m", 2, "")
+        step("s", 1, "")
+        step("m", 3, "")
+        step("s", 2, "")
+        step("s", 3, "")
+
+        hq = sb.tile([P, O], U32, name="hq", align_bytes=64)
+        hs = sb.tile([P, O], U8, name="hs", align_bytes=64)
+        nc.vector.quantize_mx(out=hq[:].bitcast(E4M3), scales=hs[:], in_=hid[:])
+
+        for h in range(N // P):
+            acc = psum.tile([P, O], F32, name="res%d" % h, tag="bank%d" % h)
+            nc.tensor.matmul_mx(out=acc[:], lhsT=wbw[:, 2 * P * h : 2 * P * (h + 1)].bitcast(E2M1),
+                                lhsT_scale=wbs[:, P * h : P * (h + 1)],
+                                rhs=hq[:].bitcast(E4M3), rhs_scale=hs[:], start=True, stop=True)
+            res = sb.tile([P, O], F32, name="res_sb%d" % h)
+            if h == 0:
+                nc.vector.tensor_copy(res[:], acc[:])
+                nc.sync.dma_start(out=out[P * h : P * (h + 1), :], in_=res[:])
+            else:
+                nc.scalar.copy(res[:], acc[:])
+                nc.scalar.dma_start(out=out[P * h : P * (h + 1), :], in_=res[:])

@@ -27,6 +27,7 @@ def tile_list_partnersig_kernel(tc, xt_words, xt_scales, w_words, w_scales, w2_w
     nc = tc.nc
     with ExitStack() as ctx:
         sb = ctx.enter_context(tc.tile_pool(name="sb", bufs=1))
+        shared = ctx.enter_context(tc.tile_pool(name="shared", bufs=1))
         psum = ctx.enter_context(tc.psum_pool(name="psum", bufs=1))
 
         def plane(name, width):
@@ -40,12 +41,13 @@ def tile_list_partnersig_kernel(tc, xt_words, xt_scales, w_words, w_scales, w2_w
 
         warm_in = sb.tile([P, 1], F32, name="warm_in")
         warm_out = sb.tile([P, 1], F32, name="warm_out")
-        nc.gpsimd.memset(warm_in[:], 0.0)
+        nc.vector.memset(warm_in[:], 0.0)
         nc.scalar.activation(out=warm_out[:], in_=warm_in[:], func=ACT.Sigmoid)
 
+        w2s = plane("w2s", 2 * R)
         xs = plane("xs", T)
-        w2s = plane("w2s", R)
-        ws = plane("ws", R)
+        ws = shared.tile([P, R], U8, name="ws", offset=768)
+        nc.vector.memset(ws[:].bitcast(I32), 0)
         wbs = plane("wbs", N)
 
         list1 = sb.tile([P, J // 16], U16, name="list1")
@@ -57,23 +59,40 @@ def tile_list_partnersig_kernel(tc, xt_words, xt_scales, w_words, w_scales, w2_w
         wbw = sb.tile([P, 2 * N], U8, name="wbw", align_bytes=64)
         slope = sb.tile([P, PACK], F32, name="slope")
         offset = sb.tile([P, PACK], F32, name="offset")
-        w2s_rows = sb.tile([4, 4, R // 4], I32, name="w2s_rows")
-        ws_rows = sb.tile([4, 4, R // 4], I32, name="ws_rows")
-        xs_rows = sb.tile([4, 4, T // 4], I32, name="xs_rows")
+
+        def load_quadrant(queue, tile_, scales, q):
+            queue.dma_start(out=tile_[32 * q : 32 * q + 4, :].bitcast(I32), in_=scales[0, 4 * q : 4 * q + 4, :].bitcast(I32))
+
+        def load_pair(queue, tile_, scales, q):
+            queue.dma_start(out=tile_[32 * q : 32 * q + 4, :].bitcast(I32).rearrange("r (u c) -> r u c", u=2),
+                            in_=scales[0].bitcast(I32).rearrange("(u q r) c -> q r u c", u=2, r=4)[q])
+
+        def lift(tile_):
+            nc.vector.tensor_copy(tile_[64:128, 0:R].bitcast(I32), tile_[0:64, R : 2 * R].bitcast(I32))
 
         nc.sync.dma_start(list1[:], offs)
-        nc.sync.dma_start(out=w2s_rows[:], in_=w2_scales[0].bitcast(I32).rearrange("(q r) c -> r q c", r=4))
         nc.sync.dma_start(out=xw[:].bitcast(I32), in_=xt_words[0].bitcast(I32))
-        nc.sync.dma_start(out=w2w[:].bitcast(I32), in_=w2_words[0].rearrange("p c t -> p (c t)").bitcast(I32))
-        load_plane(nc.sync, xs, xt_scales)
-        nc.sync.dma_start(out=ww[:].bitcast(I32), in_=w_words[0].rearrange("p c t -> p (c t)").bitcast(I32))
-        load_plane(nc.sync, ws, w_scales)
+        nc.gpsimd.dma_start(out=w2w[:].bitcast(I32), in_=w2_words[0].rearrange("p c t -> p (c t)").bitcast(I32))
+        nc.gpsimd.dma_start(out=ww[:].bitcast(I32), in_=w_words[0].rearrange("p c t -> p (c t)").bitcast(I32))
+        load_pair(nc.sync, w2s, w2_scales, 0)
+        load_pair(nc.sync, w2s, w2_scales, 1)
+        load_quadrant(nc.sync, xs, xt_scales, 0)
+        load_quadrant(nc.sync, xs, xt_scales, 1)
+        load_quadrant(nc.sync, xs, xt_scales, 2)
+        load_quadrant(nc.sync, xs, xt_scales, 3)
+        load_quadrant(nc.sync, ws, w_scales, 0)
+        load_quadrant(nc.sync, ws, w_scales, 1)
+        load_quadrant(nc.sync, ws, w_scales, 2)
+        load_quadrant(nc.sync, ws, w_scales, 3)
         nc.sync.dma_start(list2[:], offs2)
         nc.sync.dma_start(list3[:], offs3)
         nc.sync.dma_start(out=slope[:], in_=sg.rearrange("(p t) o -> p (t o)", t=PACK))
         nc.sync.dma_start(out=offset[:], in_=lo.rearrange("(p t) o -> p (t o)", t=PACK))
         nc.sync.dma_start(out=wbw[:].bitcast(I32), in_=wb_words[0].bitcast(I32))
-        load_plane(nc.sync, wbs, wb_scales)
+        load_quadrant(nc.sync, wbs, wb_scales, 0)
+        load_quadrant(nc.sync, wbs, wb_scales, 1)
+        load_quadrant(nc.sync, wbs, wb_scales, 2)
+        load_quadrant(nc.sync, wbs, wb_scales, 3)
 
         def spread(tile_, rows):
             for q in range(4):
@@ -82,6 +101,11 @@ def tile_list_partnersig_kernel(tc, xt_words, xt_scales, w_words, w_scales, w2_w
         def deal(copy, name, src, dtype):
             dealt = sb.tile([P, R], dtype, name=name, align_bytes=64)
             copy(dealt[:].rearrange("p (t m) -> p m t", t=PACK), src[:].rearrange("p (m t) -> p m t", t=PACK))
+            return dealt
+
+        def deal_bytes(name, src):
+            dealt = sb.tile([P, R], U8, name=name, align_bytes=64)
+            nc.vector.tensor_copy(dealt[:].rearrange("p (t m) -> p t m", t=PACK), src[:, 0:R].rearrange("p (m t) -> p t m", t=PACK))
             return dealt
 
         xg = sb.tile([P, J], U16, name="xg", align_bytes=64)
@@ -93,13 +117,14 @@ def tile_list_partnersig_kernel(tc, xt_words, xt_scales, w_words, w_scales, w2_w
             nc.vector.tensor_copy(xg[:, cols], xw[:].indirect(entries))
             nc.vector.tensor_copy(xsg[:, cols], xs[:].indirect(entries))
 
-        spread(w2s, w2s_rows)
-        w2s_d = deal(nc.vector.tensor_copy, "w2s_d", w2s, U8)
+        nc.vector.tensor_copy(xg[:], xw[:].indirect(list1[:]))
+        lift(w2s)
+        nc.vector.tensor_copy(xsg[:, 0:HALF], xs[:].indirect(list1[:, 0:8]))
+        w2s_d = deal_bytes("w2s_d", w2s)
+        nc.vector.tensor_copy(xsg[:, HALF:J], xs[:].indirect(list1[:, 8:16]))
         w2w_d = deal(nc.scalar.copy, "w2w_d", w2w, U32)
-        pick(0, 2)
-        pick(1, 2)
         ww_d = deal(nc.scalar.copy, "ww_d", ww, U32)
-        ws_d = deal(nc.vector.tensor_copy, "ws_d", ws, U8)
+        ws_d = deal_bytes("ws_d", ws)
 
         b_ps = [psum.tile([P, J], F32, name="bank%d" % t, tag="bank%d" % t) for t in range(PACK)]
         a_ps = [psum.tile([P, J], F32, name="bank%d" % (PACK + t), tag="bank%d" % (PACK + t)) for t in range(PACK)]
@@ -109,14 +134,15 @@ def tile_list_partnersig_kernel(tc, xt_words, xt_scales, w_words, w_scales, w2_w
             nc.tensor.matmul_mx(out=acc[:, cols], lhsT=words[:, rows].bitcast(fmt), lhsT_scale=scales[:, rows],
                                 rhs=xg[:, cols].bitcast(E2M1), rhs_scale=xsg[:, cols], start=True, stop=True)
 
-        for h in range(2):
-            for t in range(PACK):
-                product(b_ps[t], w2w_d, w2s_d, E5M2, t, slice(h * J // 2, (h + 1) * J // 2))
+        for t0 in range(0, PACK, 2):
+            for h in range(2):
+                for t in (t0, t0 + 1):
+                    product(b_ps[t], w2w_d, w2s_d, E5M2, t, slice(h * HALF, (h + 1) * HALF))
         for t in range(PACK):
             product(a_ps[t], ww_d, ws_d, E4M3, t, slice(0, J))
 
-        b_sb = [sb.tile([P, J], F32, name="b%d" % t) for t in range(PACK)]
-        partner = [sb.tile([P, J], F32, name="partner%d" % t) for t in range(PACK)]
+        b_sb = [sb.tile([P, 352], F32, name="b%d" % t) for t in range(PACK)]
+        partner = [shared.tile([P, J], F32, name="partner%d" % t, offset=[0,1024,2048,1024][t]) for t in range(PACK)]
         g1 = [sb.tile([P, J], F32, name="g1_%d" % t) for t in range(PACK)]
         hid = sb.tile([P, PACK * O], BF16, name="hid", align_bytes=64)
 
@@ -137,20 +163,16 @@ def tile_list_partnersig_kernel(tc, xt_words, xt_scales, w_words, w_scales, w2_w
                                      bias=offset[:, t : t + 1], scale=slope[:, t : t + 1])
 
         step("c", 0, "S")
-        step("c", 1, "V")
+        step("c", 1, "S")
+        step("g", 0, "V")
         step("c", 2, "S")
-        step("c", 3, "V")
-        step("h", 0, "V")
-        step("i", 0, "S")
-        step("h", 1, "V")
-        step("i", 1, "S")
+        step("g", 1, "V")
+        step("c", 3, "S")
         step("m", 0, "")
-        step("i", 2, "S")
-        step("h", 2, "V")
+        step("g", 2, "S")
         step("m", 1, "")
-        step("i", 3, "S")
-        step("h", 3, "V")
         step("s", 0, "")
+        step("g", 3, "V")
         step("m", 2, "")
         step("s", 1, "")
         step("m", 3, "")

@@ -19,7 +19,14 @@ ALU = mybir.AluOpType
 
 P = 128
 PACK = 4
+QUADRANTS = 4
+QUADRANT = P // QUADRANTS
+SCALE_ROWS = 4
+GROUP = 16
 HALF = J // 2
+LOW, HIGH, ALL = slice(0, HALF), slice(HALF, J), slice(0, J)
+B_WIDTH = 352
+ROW_BYTES = 4 * J
 
 
 def tile_list_partnersig_kernel(tc, xt_words, xt_scales, w_words, w_scales, w2_words, w2_scales, sg, lo,
@@ -30,168 +37,151 @@ def tile_list_partnersig_kernel(tc, xt_words, xt_scales, w_words, w_scales, w2_w
         shared = ctx.enter_context(tc.tile_pool(name="shared", bufs=1))
         psum = ctx.enter_context(tc.psum_pool(name="psum", bufs=1))
 
-        def plane(name, width):
-            tile_ = sb.tile([P, width], U8, name=name, align_bytes=64)
-            nc.vector.memset(tile_[:].bitcast(I32), 0)
-            return tile_
-
-        def load_plane(queue, tile_, scales):
-            for q in range(4):
-                queue.dma_start(out=tile_[32 * q : 32 * q + 4, :].bitcast(I32), in_=scales[0, 4 * q : 4 * q + 4, :].bitcast(I32))
-
         warm_in = sb.tile([P, 1], F32, name="warm_in")
         warm_out = sb.tile([P, 1], F32, name="warm_out")
         nc.vector.memset(warm_in[:], 0.0)
         nc.scalar.activation(out=warm_out[:], in_=warm_in[:], func=ACT.Sigmoid)
 
-        w2s = plane("w2s", 2 * R)
-        xs = plane("xs", T)
-        ws = shared.tile([P, R], U8, name="ws", offset=768)
-        nc.vector.memset(ws[:].bitcast(I32), 0)
-        wbs = plane("wbs", N)
+        x_scale = sb.tile([P, T], U8, name="x_scale", align_bytes=64)
+        w2_scale = sb.tile([P, R], U8, name="w2_scale", align_bytes=64)
+        w_scale = shared.tile([P, R], U8, name="w_scale", offset=ROW_BYTES - R // 2)
+        wb_scale = sb.tile([P, N], U8, name="wb_scale", align_bytes=64)
+        for scale_tile in (x_scale, w2_scale, w_scale, wb_scale):
+            nc.vector.memset(scale_tile[:].bitcast(I32), 0)
 
-        list1 = sb.tile([P, J // 16], U16, name="list1")
-        list2 = sb.tile([P, J // 16], U16, name="list2")
-        list3 = sb.tile([P, O // 16], U16, name="list3")
-        xw = sb.tile([P, T], U16, name="xw", align_bytes=64)
-        ww = sb.tile([P, R], U32, name="ww", align_bytes=64)
-        w2w = sb.tile([P, R], U32, name="w2w", align_bytes=64)
-        wbw = sb.tile([P, 2 * N], U8, name="wbw", align_bytes=64)
+        tokens = sb.tile([P, J // GROUP], U16, name="tokens")
+        partners = sb.tile([P, J // GROUP], U16, name="partners")
+        places = sb.tile([P, O // GROUP], U16, name="places")
+        x_word = sb.tile([P, T], U16, name="x_word", align_bytes=64)
+        w_word = sb.tile([P, R], U32, name="w_word", align_bytes=64)
+        w2_word = sb.tile([P, R], U32, name="w2_word", tag="w2_then_w", align_bytes=64)
+        wb_word = sb.tile([P, 2 * N], U8, name="wb_word", align_bytes=64)
         slope = sb.tile([P, PACK], F32, name="slope")
-        offset = sb.tile([P, PACK], F32, name="offset")
+        shift = sb.tile([P, PACK], F32, name="shift")
+        w2_rows = sb.tile([SCALE_ROWS, QUADRANTS, R // 4], I32, name="w2_rows")
 
-        def load_quadrant(queue, tile_, scales, q):
-            queue.dma_start(out=tile_[32 * q : 32 * q + 4, :].bitcast(I32), in_=scales[0, 4 * q : 4 * q + 4, :].bitcast(I32))
+        def quadrant_rows(scale_tile, q):
+            return scale_tile[QUADRANT * q : QUADRANT * q + SCALE_ROWS, :].bitcast(I32)
 
-        def load_pair(queue, tile_, scales, q):
-            queue.dma_start(out=tile_[32 * q : 32 * q + 4, :].bitcast(I32).rearrange("r (u c) -> r u c", u=2),
-                            in_=scales[0].bitcast(I32).rearrange("(u q r) c -> q r u c", u=2, r=4)[q])
+        def load_scales(scale_tile, scales, quadrants):
+            for q in quadrants:
+                rows = scales[0, SCALE_ROWS * q : SCALE_ROWS * (q + 1), :]
+                nc.sync.dma_start(out=quadrant_rows(scale_tile, q), in_=rows.bitcast(I32))
 
-        def lift(tile_):
-            nc.vector.tensor_copy(tile_[64:128, 0:R].bitcast(I32), tile_[0:64, R : 2 * R].bitcast(I32))
+        def fp8_words(words):
+            return words[0].rearrange("p c t -> p (c t)").bitcast(I32)
 
-        nc.sync.dma_start(list1[:], offs)
-        nc.sync.dma_start(out=xw[:].bitcast(I32), in_=xt_words[0].bitcast(I32))
-        nc.gpsimd.dma_start(out=w2w[:].bitcast(I32), in_=w2_words[0].rearrange("p c t -> p (c t)").bitcast(I32))
-        nc.gpsimd.dma_start(out=ww[:].bitcast(I32), in_=w_words[0].rearrange("p c t -> p (c t)").bitcast(I32))
-        load_pair(nc.sync, w2s, w2_scales, 0)
-        load_pair(nc.sync, w2s, w2_scales, 1)
-        load_quadrant(nc.sync, xs, xt_scales, 0)
-        load_quadrant(nc.sync, xs, xt_scales, 1)
-        load_quadrant(nc.sync, xs, xt_scales, 2)
-        load_quadrant(nc.sync, xs, xt_scales, 3)
-        load_quadrant(nc.sync, ws, w_scales, 0)
-        load_quadrant(nc.sync, ws, w_scales, 1)
-        load_quadrant(nc.sync, ws, w_scales, 2)
-        load_quadrant(nc.sync, ws, w_scales, 3)
-        nc.sync.dma_start(list2[:], offs2)
-        nc.sync.dma_start(list3[:], offs3)
+        nc.sync.dma_start(tokens[:], offs)
+        nc.sync.dma_start(out=w2_rows[:], in_=w2_scales[0].bitcast(I32).rearrange("(q s) c -> s q c", s=SCALE_ROWS))
+        nc.sync.dma_start(out=x_word[:].bitcast(I32), in_=xt_words[0].bitcast(I32))
+        load_scales(x_scale, xt_scales, range(0, 1))
+        nc.sync.dma_start(out=w2_word[:].bitcast(I32), in_=fp8_words(w2_words))
+        nc.gpsimd.dma_start(out=w_word[:].bitcast(I32), in_=fp8_words(w_words))
+        load_scales(x_scale, xt_scales, range(1, QUADRANTS))
+        load_scales(w_scale, w_scales, range(QUADRANTS))
+        nc.sync.dma_start(partners[:], offs2)
+        nc.sync.dma_start(places[:], offs3)
         nc.sync.dma_start(out=slope[:], in_=sg.rearrange("(p t) o -> p (t o)", t=PACK))
-        nc.sync.dma_start(out=offset[:], in_=lo.rearrange("(p t) o -> p (t o)", t=PACK))
-        nc.sync.dma_start(out=wbw[:].bitcast(I32), in_=wb_words[0].bitcast(I32))
-        load_quadrant(nc.sync, wbs, wb_scales, 0)
-        load_quadrant(nc.sync, wbs, wb_scales, 1)
-        load_quadrant(nc.sync, wbs, wb_scales, 2)
-        load_quadrant(nc.sync, wbs, wb_scales, 3)
+        nc.sync.dma_start(out=shift[:], in_=lo.rearrange("(p t) o -> p (t o)", t=PACK))
+        nc.sync.dma_start(out=wb_word[:].bitcast(I32), in_=wb_words[0].bitcast(I32))
+        load_scales(wb_scale, wb_scales, range(QUADRANTS))
 
-        def spread(tile_, rows):
-            for q in range(4):
-                nc.vector.tensor_copy(tile_[32 * q : 32 * q + 4, :].bitcast(I32), rows[:, q, :])
-
-        def deal(copy, name, src, dtype):
-            dealt = sb.tile([P, R], dtype, name=name, align_bytes=64)
-            copy(dealt[:].rearrange("p (t m) -> p m t", t=PACK), src[:].rearrange("p (m t) -> p m t", t=PACK))
+        def deal_words(name, tag, words):
+            dealt = sb.tile([P, R], U32, name=name, tag=tag, align_bytes=64)
+            nc.scalar.copy(dealt[:].rearrange("p (t m) -> p m t", t=PACK), words[:].rearrange("p (m t) -> p m t", t=PACK))
             return dealt
 
-        def deal_bytes(name, src):
+        def deal_scales(name, scale_tile):
             dealt = sb.tile([P, R], U8, name=name, align_bytes=64)
-            nc.vector.tensor_copy(dealt[:].rearrange("p (t m) -> p t m", t=PACK), src[:, 0:R].rearrange("p (m t) -> p t m", t=PACK))
+            nc.vector.tensor_copy(dealt[:].rearrange("p (t m) -> p t m", t=PACK),
+                                  scale_tile[:].rearrange("p (m t) -> p t m", t=PACK))
             return dealt
 
-        xg = sb.tile([P, J], U16, name="xg", align_bytes=64)
-        xsg = sb.tile([P, J], U8, name="xsg", align_bytes=64)
+        def entries(list_tile, slots):
+            return list_tile[:, slots.start // GROUP : slots.stop // GROUP]
 
-        def pick(h, n):
-            cols = slice(h * J // n, (h + 1) * J // n)
-            entries = list1[:, h * 16 // n : (h + 1) * 16 // n]
-            nc.vector.tensor_copy(xg[:, cols], xw[:].indirect(entries))
-            nc.vector.tensor_copy(xsg[:, cols], xs[:].indirect(entries))
+        for q in range(QUADRANTS):
+            nc.vector.tensor_copy(quadrant_rows(w2_scale, q), w2_rows[:, q, :])
 
-        nc.vector.tensor_copy(xg[:], xw[:].indirect(list1[:]))
-        lift(w2s)
-        nc.vector.tensor_copy(xsg[:, 0:HALF], xs[:].indirect(list1[:, 0:8]))
-        w2s_d = deal_bytes("w2s_d", w2s)
-        nc.vector.tensor_copy(xsg[:, HALF:J], xs[:].indirect(list1[:, 8:16]))
-        w2w_d = deal(nc.scalar.copy, "w2w_d", w2w, U32)
-        ww_d = deal(nc.scalar.copy, "ww_d", ww, U32)
-        ws_d = deal_bytes("ws_d", ws)
+        picked_word = sb.tile([P, J], U16, name="picked_word", align_bytes=64)
+        picked_scale = sb.tile([P, J], U8, name="picked_scale", align_bytes=64)
+        nc.vector.tensor_copy(picked_word[:], x_word[:].indirect(tokens[:]))
+        w2_scale_dealt = deal_scales("w2_scale_dealt", w2_scale)
+        for slots in (LOW, HIGH):
+            nc.vector.tensor_copy(picked_scale[:, slots], x_scale[:].indirect(entries(tokens, slots)))
+        w2_word_dealt = deal_words("w2_word_dealt", "w2_word_dealt", w2_word)
+        w_word_dealt = deal_words("w_word_dealt", "w2_then_w", w_word)
+        w_scale_dealt = deal_scales("w_scale_dealt", w_scale)
 
-        b_ps = [psum.tile([P, J], F32, name="bank%d" % t, tag="bank%d" % t) for t in range(PACK)]
-        a_ps = [psum.tile([P, J], F32, name="bank%d" % (PACK + t), tag="bank%d" % (PACK + t)) for t in range(PACK)]
+        b_psum = [psum.tile([P, J], F32, name="b_psum%d" % t, tag="bank%d" % t) for t in range(PACK)]
+        a_psum = [psum.tile([P, J], F32, name="a_psum%d" % t, tag="bank%d" % (PACK + t)) for t in range(PACK)]
 
-        def product(acc, words, scales, fmt, t, cols):
-            rows = slice(t * P, (t + 1) * P)
-            nc.tensor.matmul_mx(out=acc[:, cols], lhsT=words[:, rows].bitcast(fmt), lhsT_scale=scales[:, rows],
-                                rhs=xg[:, cols].bitcast(E2M1), rhs_scale=xsg[:, cols], start=True, stop=True)
+        def product(acc, words, scales, fmt, t, slots):
+            cols = slice(t * P, (t + 1) * P)
+            nc.tensor.matmul_mx(out=acc[:, slots], lhsT=words[:, cols].bitcast(fmt), lhsT_scale=scales[:, cols],
+                                rhs=picked_word[:, slots].bitcast(E2M1), rhs_scale=picked_scale[:, slots],
+                                start=True, stop=True)
 
-        for t0 in range(0, PACK, 2):
-            for h in range(2):
-                for t in (t0, t0 + 1):
-                    product(b_ps[t], w2w_d, w2s_d, E5M2, t, slice(h * HALF, (h + 1) * HALF))
+        for first in range(0, PACK, 2):
+            for slots in (LOW, HIGH):
+                for t in (first, first + 1):
+                    product(b_psum[t], w2_word_dealt, w2_scale_dealt, E5M2, t, slots)
         for t in range(PACK):
-            product(a_ps[t], ww_d, ws_d, E4M3, t, slice(0, J))
+            product(a_psum[t], w_word_dealt, w_scale_dealt, E4M3, t, ALL)
 
-        b_sb = [sb.tile([P, 352], F32, name="b%d" % t) for t in range(PACK)]
-        partner = [shared.tile([P, J], F32, name="partner%d" % t, offset=[0,1024,2048,1024][t]) for t in range(PACK)]
+        b = [sb.tile([P, B_WIDTH], F32, name="b%d" % t) for t in range(PACK)]
         g1 = [sb.tile([P, J], F32, name="g1_%d" % t) for t in range(PACK)]
         hid = sb.tile([P, PACK * O], BF16, name="hid", align_bytes=64)
 
-        def step(kind, t, eng):
-            if kind == "c":
-                (nc.vector.tensor_copy if eng == "V" else nc.scalar.copy)(b_sb[t][:, 0:J], b_ps[t][:])
-            elif kind in ("g", "h", "i"):
-                lo_, hi_ = {"g": (0, J), "h": (0, HALF), "i": (HALF, J)}[kind]
-                src = b_sb[t][:].indirect(list2[:, lo_ // 16 : hi_ // 16])
-                if eng == "V":
-                    nc.vector.tensor_copy(partner[t][:, lo_:hi_], src)
-                else:
-                    nc.scalar.activation(partner[t][:, lo_:hi_], src, ACT.Copy)
-            elif kind == "m":
-                nc.vector.tensor_tensor(g1[t][:], a_ps[t][:], partner[t][:], ALU.max)
-            else:
-                nc.scalar.activation(out=hid[:, t : PACK * O : PACK], in_=g1[t][:].indirect(list3[:]), func=ACT.Sigmoid,
-                                     bias=offset[:, t : t + 1], scale=slope[:, t : t + 1])
+        last = PACK - 1
+        partner = [shared.tile([P, J], F32, name="partner%d" % t, offset=t * ROW_BYTES) for t in range(last)]
+        last_high = shared.tile([P, HALF], F32, name="last_high", offset=last * ROW_BYTES)
+        last_low = shared.tile([P, HALF], F32, name="last_low", offset=ROW_BYTES)
 
-        step("c", 0, "S")
-        step("c", 1, "S")
-        step("g", 0, "V")
-        step("c", 2, "S")
-        step("g", 1, "V")
-        step("c", 3, "S")
-        step("m", 0, "")
-        step("g", 2, "S")
-        step("m", 1, "")
-        step("s", 0, "")
-        step("g", 3, "V")
-        step("m", 2, "")
-        step("s", 1, "")
-        step("m", 3, "")
-        step("s", 2, "")
-        step("s", 3, "")
+        def copy_b(t):
+            nc.scalar.copy(b[t][:, ALL], b_psum[t][:])
 
-        hq = sb.tile([P, O], U32, name="hq", align_bytes=64)
-        hs = sb.tile([P, O], U8, name="hs", align_bytes=64)
-        nc.vector.quantize_mx(out=hq[:].bitcast(E4M3), scales=hs[:], in_=hid[:])
+        def look_up_on_vector(dst, t, slots):
+            nc.vector.tensor_copy(dst[:], b[t][:].indirect(entries(partners, slots)))
 
-        for h in range(N // P):
-            acc = psum.tile([P, O], F32, name="res%d" % h, tag="bank%d" % h)
-            nc.tensor.matmul_mx(out=acc[:], lhsT=wbw[:, 2 * P * h : 2 * P * (h + 1)].bitcast(E2M1),
-                                lhsT_scale=wbs[:, P * h : P * (h + 1)],
-                                rhs=hq[:].bitcast(E4M3), rhs_scale=hs[:], start=True, stop=True)
-            res = sb.tile([P, O], F32, name="res_sb%d" % h)
-            if h == 0:
-                nc.vector.tensor_copy(res[:], acc[:])
-                nc.sync.dma_start(out=out[P * h : P * (h + 1), :], in_=res[:])
-            else:
-                nc.scalar.copy(res[:], acc[:])
-                nc.scalar.dma_start(out=out[P * h : P * (h + 1), :], in_=res[:])
+        def look_up_on_scalar(dst, t, slots):
+            nc.scalar.activation(dst[:], b[t][:].indirect(entries(partners, slots)), ACT.Copy)
+
+        def keep_larger(t, slots, other):
+            nc.vector.tensor_tensor(g1[t][:, slots], a_psum[t][:, slots], other[:], ALU.max)
+
+        def fetch_hid(t):
+            nc.scalar.activation(out=hid[:, t : PACK * O : PACK], in_=g1[t][:].indirect(places[:]), func=ACT.Sigmoid,
+                                 bias=shift[:, t : t + 1], scale=slope[:, t : t + 1])
+
+        copy_b(0)
+        copy_b(1)
+        look_up_on_vector(partner[0], 0, ALL)
+        copy_b(2)
+        look_up_on_vector(partner[1], 1, ALL)
+        copy_b(last)
+        keep_larger(0, ALL, partner[0])
+        look_up_on_scalar(partner[2], 2, ALL)
+        keep_larger(1, ALL, partner[1])
+        look_up_on_scalar(last_high, last, HIGH)
+        fetch_hid(0)
+        look_up_on_vector(last_low, last, LOW)
+        keep_larger(2, ALL, partner[2])
+        fetch_hid(1)
+        keep_larger(last, HIGH, last_high)
+        keep_larger(last, LOW, last_low)
+        fetch_hid(2)
+        fetch_hid(last)
+
+        hid_word = sb.tile([P, O], U32, name="hid_word", align_bytes=64)
+        hid_scale = sb.tile([P, O], U8, name="hid_scale", align_bytes=64)
+        nc.vector.quantize_mx(out=hid_word[:].bitcast(E4M3), scales=hid_scale[:], in_=hid[:])
+
+        for h, (copy, queue) in enumerate(((nc.vector.tensor_copy, nc.sync), (nc.scalar.copy, nc.scalar))):
+            out_psum = psum.tile([P, O], F32, name="out_psum%d" % h, tag="bank%d" % h)
+            nc.tensor.matmul_mx(out=out_psum[:], lhsT=wb_word[:, 2 * P * h : 2 * P * (h + 1)].bitcast(E2M1),
+                                lhsT_scale=wb_scale[:, P * h : P * (h + 1)],
+                                rhs=hid_word[:].bitcast(E4M3), rhs_scale=hid_scale[:], start=True, stop=True)
+            result = sb.tile([P, O], F32, name="result%d" % h)
+            copy(result[:], out_psum[:])
+            queue.dma_start(out=out[P * h : P * (h + 1), :], in_=result[:])

@@ -42,11 +42,11 @@ def tile_list_partnersig_kernel(tc, xt_words, xt_scales, w_words, w_scales, w2_w
         nc.vector.memset(warm_in[:], 0.0)
         nc.scalar.activation(out=warm_out[:], in_=warm_in[:], func=ACT.Sigmoid)
 
+        w2_scale = sb.tile([P, 2 * R], U8, name="w2_scale", align_bytes=64)
         x_scale = sb.tile([P, T], U8, name="x_scale", align_bytes=64)
-        w2_scale = sb.tile([P, R], U8, name="w2_scale", align_bytes=64)
         w_scale = shared.tile([P, R], U8, name="w_scale", offset=ROW_BYTES - R // 2)
         wb_scale = sb.tile([P, N], U8, name="wb_scale", align_bytes=64)
-        for scale_tile in (x_scale, w2_scale, w_scale, wb_scale):
+        for scale_tile in (w2_scale, x_scale, w_scale, wb_scale):
             nc.vector.memset(scale_tile[:].bitcast(I32), 0)
 
         tokens = sb.tile([P, J // GROUP], U16, name="tokens")
@@ -58,13 +58,12 @@ def tile_list_partnersig_kernel(tc, xt_words, xt_scales, w_words, w_scales, w2_w
         wb_word = sb.tile([P, 2 * N], U8, name="wb_word", align_bytes=64)
         slope = sb.tile([P, PACK], F32, name="slope")
         shift = sb.tile([P, PACK], F32, name="shift")
-        w2_rows = sb.tile([SCALE_ROWS, QUADRANTS, R // 4], I32, name="w2_rows")
 
         def quadrant_rows(scale_tile, q):
             return scale_tile[QUADRANT * q : QUADRANT * q + SCALE_ROWS, :].bitcast(I32)
 
-        def load_scales(scale_tile, scales, quadrants):
-            for q in quadrants:
+        def load_scales(scale_tile, scales):
+            for q in range(QUADRANTS):
                 rows = scales[0, SCALE_ROWS * q : SCALE_ROWS * (q + 1), :]
                 nc.sync.dma_start(out=quadrant_rows(scale_tile, q), in_=rows.bitcast(I32))
 
@@ -72,19 +71,20 @@ def tile_list_partnersig_kernel(tc, xt_words, xt_scales, w_words, w_scales, w2_w
             return words[0].rearrange("p c t -> p (c t)").bitcast(I32)
 
         nc.sync.dma_start(tokens[:], offs)
-        nc.sync.dma_start(out=w2_rows[:], in_=w2_scales[0].bitcast(I32).rearrange("(q s) c -> s q c", s=SCALE_ROWS))
         nc.sync.dma_start(out=x_word[:].bitcast(I32), in_=xt_words[0].bitcast(I32))
-        load_scales(x_scale, xt_scales, range(0, 1))
-        nc.sync.dma_start(out=w2_word[:].bitcast(I32), in_=fp8_words(w2_words))
+        nc.gpsimd.dma_start(out=w2_word[:].bitcast(I32), in_=fp8_words(w2_words))
         nc.gpsimd.dma_start(out=w_word[:].bitcast(I32), in_=fp8_words(w_words))
-        load_scales(x_scale, xt_scales, range(1, QUADRANTS))
-        load_scales(w_scale, w_scales, range(QUADRANTS))
+        w2_row_pairs = w2_scales[0].bitcast(I32).rearrange("(u q s) c -> q s u c", u=2, s=SCALE_ROWS)
+        for q in range(QUADRANTS // 2):
+            nc.sync.dma_start(out=quadrant_rows(w2_scale, q).rearrange("s (u c) -> s u c", u=2), in_=w2_row_pairs[q])
+        load_scales(x_scale, xt_scales)
+        load_scales(w_scale, w_scales)
         nc.sync.dma_start(partners[:], offs2)
         nc.sync.dma_start(places[:], offs3)
         nc.sync.dma_start(out=slope[:], in_=sg.rearrange("(p t) o -> p (t o)", t=PACK))
         nc.sync.dma_start(out=shift[:], in_=lo.rearrange("(p t) o -> p (t o)", t=PACK))
         nc.sync.dma_start(out=wb_word[:].bitcast(I32), in_=wb_words[0].bitcast(I32))
-        load_scales(wb_scale, wb_scales, range(QUADRANTS))
+        load_scales(wb_scale, wb_scales)
 
         def deal_words(name, tag, words):
             dealt = sb.tile([P, R], U32, name=name, tag=tag, align_bytes=64)
@@ -94,21 +94,19 @@ def tile_list_partnersig_kernel(tc, xt_words, xt_scales, w_words, w_scales, w2_w
         def deal_scales(name, scale_tile):
             dealt = sb.tile([P, R], U8, name=name, align_bytes=64)
             nc.vector.tensor_copy(dealt[:].rearrange("p (t m) -> p t m", t=PACK),
-                                  scale_tile[:].rearrange("p (m t) -> p t m", t=PACK))
+                                  scale_tile[:, 0:R].rearrange("p (m t) -> p t m", t=PACK))
             return dealt
 
         def entries(list_tile, slots):
             return list_tile[:, slots.start // GROUP : slots.stop // GROUP]
 
-        for q in range(QUADRANTS):
-            nc.vector.tensor_copy(quadrant_rows(w2_scale, q), w2_rows[:, q, :])
-
         picked_word = sb.tile([P, J], U16, name="picked_word", align_bytes=64)
         picked_scale = sb.tile([P, J], U8, name="picked_scale", align_bytes=64)
         nc.vector.tensor_copy(picked_word[:], x_word[:].indirect(tokens[:]))
+        nc.vector.tensor_copy(w2_scale[P // 2 : P, 0:R].bitcast(I32), w2_scale[0 : P // 2, R : 2 * R].bitcast(I32))
+        nc.vector.tensor_copy(picked_scale[:, LOW], x_scale[:].indirect(entries(tokens, LOW)))
         w2_scale_dealt = deal_scales("w2_scale_dealt", w2_scale)
-        for slots in (LOW, HIGH):
-            nc.vector.tensor_copy(picked_scale[:, slots], x_scale[:].indirect(entries(tokens, slots)))
+        nc.vector.tensor_copy(picked_scale[:, HIGH], x_scale[:].indirect(entries(tokens, HIGH)))
         w2_word_dealt = deal_words("w2_word_dealt", "w2_word_dealt", w2_word)
         w_word_dealt = deal_words("w_word_dealt", "w2_then_w", w_word)
         w_scale_dealt = deal_scales("w_scale_dealt", w_scale)

from contextlib import ExitStack

import concourse.mybir as mybir

K, T, J, R, O, N = 512, 1024, 256, 512, 128, 256
FLOPS = 2 * K * R * J * 2 + 2 * R * N * O

F32 = mybir.dt.float32
BF16 = mybir.dt.bfloat16
I32 = mybir.dt.int32
U32 = mybir.dt.uint32
U16 = mybir.dt.uint16
U8 = mybir.dt.uint8
E4M3 = mybir.dt.float8_e4m3fn_x4
E5M2 = mybir.dt.float8_e5m2_x4
E2M1 = mybir.dt.float4_e2m1fn_x4
ACT = mybir.ActivationFunctionType
ALU = mybir.AluOpType

P = 128
PACK = 4
QUADRANTS = 4
QUADRANT = P // QUADRANTS
SCALE_ROWS = 4
GROUP = 16
HALF = J // 2
LOW, HIGH, ALL = slice(0, HALF), slice(HALF, J), slice(0, J)
B_WIDTH = 352
ROW_BYTES = 4 * J


def tile_list_partnersig_kernel(tc, xt_words, xt_scales, w_words, w_scales, w2_words, w2_scales, sg, lo,
                                    wb_words, wb_scales, offs, offs2, offs3, out):
    nc = tc.nc
    with ExitStack() as ctx:
        sb = ctx.enter_context(tc.tile_pool(name="sb", bufs=1))
        shared = ctx.enter_context(tc.tile_pool(name="shared", bufs=1))
        psum = ctx.enter_context(tc.psum_pool(name="psum", bufs=1))

        warm_in = sb.tile([P, 1], F32, name="warm_in")
        warm_out = sb.tile([P, 1], F32, name="warm_out")
        nc.vector.memset(warm_in[:], 0.0)
        nc.scalar.activation(out=warm_out[:], in_=warm_in[:], func=ACT.Sigmoid)

        w2_scale = sb.tile([P, 2 * R], U8, name="w2_scale", align_bytes=64)
        x_scale = sb.tile([P, T], U8, name="x_scale", align_bytes=64)
        w_scale = shared.tile([P, R], U8, name="w_scale", offset=ROW_BYTES - R // 2)
        wb_scale = sb.tile([P, N], U8, name="wb_scale", align_bytes=64)
        for scale_tile in (w2_scale, x_scale, w_scale, wb_scale):
            nc.vector.memset(scale_tile[:].bitcast(I32), 0)

        tokens = sb.tile([P, J // GROUP], U16, name="tokens")
        partners = sb.tile([P, J // GROUP], U16, name="partners")
        places = sb.tile([P, O // GROUP], U16, name="places")
        x_word = sb.tile([P, T], U16, name="x_word", align_bytes=64)
        w_word = sb.tile([P, R], U32, name="w_word", align_bytes=64)
        w2_word = sb.tile([P, R], U32, name="w2_word", tag="w2_then_w", align_bytes=64)
        wb_word = sb.tile([P, 2 * N], U8, name="wb_word", align_bytes=64)
        slope = sb.tile([P, PACK], F32, name="slope")
        shift = sb.tile([P, PACK], F32, name="shift")

        def quadrant_rows(scale_tile, q):
            return scale_tile[QUADRANT * q : QUADRANT * q + SCALE_ROWS, :].bitcast(I32)

        def load_scales(scale_tile, scales):
            for q in range(QUADRANTS):
                rows = scales[0, SCALE_ROWS * q : SCALE_ROWS * (q + 1), :]
                nc.sync.dma_start(out=quadrant_rows(scale_tile, q), in_=rows.bitcast(I32))

        def fp8_words(words):
            return words[0].rearrange("p c t -> p (c t)").bitcast(I32)

        nc.sync.dma_start(tokens[:], offs)
        nc.sync.dma_start(out=x_word[:].bitcast(I32), in_=xt_words[0].bitcast(I32))
        nc.gpsimd.dma_start(out=w2_word[:].bitcast(I32), in_=fp8_words(w2_words))
        nc.gpsimd.dma_start(out=w_word[:].bitcast(I32), in_=fp8_words(w_words))
        w2_row_pairs = w2_scales[0].bitcast(I32).rearrange("(u q s) c -> q s u c", u=2, s=SCALE_ROWS)
        for q in range(QUADRANTS // 2):
            nc.sync.dma_start(out=quadrant_rows(w2_scale, q).rearrange("s (u c) -> s u c", u=2), in_=w2_row_pairs[q])
        load_scales(x_scale, xt_scales)
        load_scales(w_scale, w_scales)
        nc.sync.dma_start(partners[:], offs2)
        nc.sync.dma_start(places[:], offs3)
        nc.sync.dma_start(out=slope[:], in_=sg.rearrange("(p t) o -> p (t o)", t=PACK))
        nc.sync.dma_start(out=shift[:], in_=lo.rearrange("(p t) o -> p (t o)", t=PACK))
        nc.sync.dma_start(out=wb_word[:].bitcast(I32), in_=wb_words[0].bitcast(I32))
        load_scales(wb_scale, wb_scales)

        def deal_words(name, tag, words):
            dealt = sb.tile([P, R], U32, name=name, tag=tag, align_bytes=64)
            nc.scalar.copy(dealt[:].rearrange("p (t m) -> p m t", t=PACK), words[:].rearrange("p (m t) -> p m t", t=PACK))
            return dealt

        def deal_scales(name, scale_tile):
            dealt = sb.tile([P, R], U8, name=name, align_bytes=64)
            nc.vector.tensor_copy(dealt[:].rearrange("p (t m) -> p t m", t=PACK),
                                  scale_tile[:, 0:R].rearrange("p (m t) -> p t m", t=PACK))
            return dealt

        def entries(list_tile, slots):
            return list_tile[:, slots.start // GROUP : slots.stop // GROUP]

        picked_word = sb.tile([P, J], U16, name="picked_word", align_bytes=64)
        picked_scale = sb.tile([P, J], U8, name="picked_scale", align_bytes=64)
        nc.vector.tensor_copy(picked_word[:], x_word[:].indirect(tokens[:]))
        nc.vector.tensor_copy(w2_scale[P // 2 : P, 0:R].bitcast(I32), w2_scale[0 : P // 2, R : 2 * R].bitcast(I32))
        nc.vector.tensor_copy(picked_scale[:, LOW], x_scale[:].indirect(entries(tokens, LOW)))
        w2_scale_dealt = deal_scales("w2_scale_dealt", w2_scale)
        nc.vector.tensor_copy(picked_scale[:, HIGH], x_scale[:].indirect(entries(tokens, HIGH)))
        w2_word_dealt = deal_words("w2_word_dealt", "w2_word_dealt", w2_word)
        w_word_dealt = deal_words("w_word_dealt", "w2_then_w", w_word)
        w_scale_dealt = deal_scales("w_scale_dealt", w_scale)

        b_psum = [psum.tile([P, J], F32, name="b_psum%d" % t, tag="bank%d" % t) for t in range(PACK)]
        a_psum = [psum.tile([P, J], F32, name="a_psum%d" % t, tag="bank%d" % (PACK + t)) for t in range(PACK)]

        def product(acc, words, scales, fmt, t, slots):
            cols = slice(t * P, (t + 1) * P)
            nc.tensor.matmul_mx(out=acc[:, slots], lhsT=words[:, cols].bitcast(fmt), lhsT_scale=scales[:, cols],
                                rhs=picked_word[:, slots].bitcast(E2M1), rhs_scale=picked_scale[:, slots],
                                start=True, stop=True)

        for first in range(0, PACK, 2):
            for slots in (LOW, HIGH):
                for t in (first, first + 1):
                    product(b_psum[t], w2_word_dealt, w2_scale_dealt, E5M2, t, slots)
        for t in range(PACK):
            product(a_psum[t], w_word_dealt, w_scale_dealt, E4M3, t, ALL)

        b = [sb.tile([P, B_WIDTH], F32, name="b%d" % t) for t in range(PACK)]
        g1 = [sb.tile([P, J], F32, name="g1_%d" % t) for t in range(PACK)]
        hid = sb.tile([P, PACK * O], BF16, name="hid", align_bytes=64)

        last = PACK - 1
        partner = [shared.tile([P, J], F32, name="partner%d" % t, offset=t * ROW_BYTES) for t in range(last)]
        last_high = shared.tile([P, HALF], F32, name="last_high", offset=last * ROW_BYTES)
        last_low = shared.tile([P, HALF], F32, name="last_low", offset=ROW_BYTES)

        def copy_b(t):
            nc.scalar.copy(b[t][:, ALL], b_psum[t][:])

        def look_up_on_vector(dst, t, slots):
            nc.vector.tensor_copy(dst[:], b[t][:].indirect(entries(partners, slots)))

        def look_up_on_scalar(dst, t, slots):
            nc.scalar.activation(dst[:], b[t][:].indirect(entries(partners, slots)), ACT.Copy)

        def keep_larger(t, slots, other):
            nc.vector.tensor_tensor(g1[t][:, slots], a_psum[t][:, slots], other[:], ALU.max)

        def fetch_hid(t):
            nc.scalar.activation(out=hid[:, t : PACK * O : PACK], in_=g1[t][:].indirect(places[:]), func=ACT.Sigmoid,
                                 bias=shift[:, t : t + 1], scale=slope[:, t : t + 1])

        copy_b(0)
        copy_b(1)
        look_up_on_vector(partner[0], 0, ALL)
        copy_b(2)
        look_up_on_vector(partner[1], 1, ALL)
        copy_b(last)
        keep_larger(0, ALL, partner[0])
        look_up_on_scalar(partner[2], 2, ALL)
        keep_larger(1, ALL, partner[1])
        look_up_on_scalar(last_high, last, HIGH)
        fetch_hid(0)
        look_up_on_vector(last_low, last, LOW)
        keep_larger(2, ALL, partner[2])
        fetch_hid(1)
        keep_larger(last, HIGH, last_high)
        keep_larger(last, LOW, last_low)
        fetch_hid(2)
        fetch_hid(last)

        hid_word = sb.tile([P, O], U32, name="hid_word", align_bytes=64)
        hid_scale = sb.tile([P, O], U8, name="hid_scale", align_bytes=64)
        nc.vector.quantize_mx(out=hid_word[:].bitcast(E4M3), scales=hid_scale[:], in_=hid[:])

        for h, (copy, queue) in enumerate(((nc.vector.tensor_copy, nc.sync), (nc.scalar.copy, nc.scalar))):
            out_psum = psum.tile([P, O], F32, name="out_psum%d" % h, tag="bank%d" % h)
            nc.tensor.matmul_mx(out=out_psum[:], lhsT=wb_word[:, 2 * P * h : 2 * P * (h + 1)].bitcast(E2M1),
                                lhsT_scale=wb_scale[:, P * h : P * (h + 1)],
                                rhs=hid_word[:].bitcast(E4M3), rhs_scale=hid_scale[:], start=True, stop=True)
            result = sb.tile([P, O], F32, name="result%d" % h)
            copy(result[:], out_psum[:])
            queue.dma_start(out=out[P * h : P * (h + 1), :], in_=result[:])
